import numpy as np
import ml_dtypes


def mxq(x, axis, fmt="e4m3"):
    dtype, down = {"e4m3": (ml_dtypes.float8_e4m3fn, 7), "e5m2": (ml_dtypes.float8_e5m2, 14)}[fmt]
    v = np.moveaxis(np.asarray(x, np.float32).astype(ml_dtypes.bfloat16).astype(np.float64), axis, -1)
    blocks = v.reshape(v.shape[:-1] + (-1, 32))
    amax = np.abs(blocks).max(-1, keepdims=True)
    byte = np.maximum(np.where(amax > 0, np.frexp(amax)[1] - 1 + 127, 0) - down, 1)
    scale = np.exp2(byte - 127.0)
    codes = (blocks / scale).astype(np.float32).astype(dtype).astype(np.float64)
    return np.moveaxis((codes * scale).reshape(v.shape), -1, axis)


WIDE = False


def mx_kscale(k):
    if not WIDE:
        return np.ones(k)
    levels = np.array([10, -10, 5, -5, 0])
    if k % 512:
        return np.exp2(np.random.permutation(np.resize(levels, k // 32))).repeat(32)
    a = np.empty((k // 512, 16))
    for p in range(k // 512):
        a[p, :8] = np.random.permutation(np.resize(levels, 8))
        for g in range(8):
            far = levels[np.abs(levels - a[p, g]) >= 10]
            a[p, g + 8] = far[np.random.randint(len(far))]
    return np.exp2(a.ravel()).repeat(32)


def f64(x):
    return np.asarray(x).astype(np.float64)


def striped(idx):
    return np.tile(idx.reshape(-1, 16).T, (8, 1)).astype(np.uint16)


def unstriped(offs):
    return offs[:16].T.reshape(-1).astype(np.int64)


def striped8(idx):
    return np.concatenate([x.reshape(-1, 16).T for x in idx]).astype(np.uint16)


def runs(offs, k):
    lists = np.stack([offs[16 * r : 16 * r + 16].T.reshape(-1) for r in range(8)]).astype(np.int64)
    return lists[np.arange(k) % 512 // 64]


def pack_weight(w):
    k, n = w.shape
    w = f64(np.asarray(w, np.float32).astype(ml_dtypes.bfloat16)).reshape(k // 32, 32, n)
    amax = np.abs(w).max(1)
    byte = np.clip(np.where(amax > 0, np.frexp(amax)[1] - 1 + 127 - 7, 1), 1, 254)
    scaled = (w * np.exp2(127.0 - byte)[:, None, :]).reshape(k, n).astype(np.float32)
    words = np.ascontiguousarray(scaled.reshape(k // 512, 128, 4, n).transpose(0, 1, 3, 2)).astype(ml_dtypes.float8_e4m3fn).view(np.uint8)
    return words, np.ascontiguousarray(byte.astype(np.uint8).reshape(k // 512, 16, n))


def unpack_weight(words, scales):
    g, p, n, _ = words.shape
    vals = np.ascontiguousarray(words).view(ml_dtypes.float8_e4m3fn).astype(np.float64) * np.repeat(np.exp2(scales.astype(np.float64) - 127.0), 8, axis=1)[..., None]
    return vals.transpose(0, 1, 3, 2).reshape(g * 512, n)


K, T, S, H, C, W = 512, 2048, 512, 512, 512, 256


def setup_inputs():
    n = np.random.standard_normal
    s = mx_kscale(K)[:, None]
    packed_xT = pack_weight(n((K, T)) * s)
    return {
        "x_words": packed_xT[0],
        "x_scales": packed_xT[1],
        "w1": (n((K, H)) / np.sqrt(K) / s).astype(np.float32),
        "gs": (np.random.uniform(0.5, 1.5, (K, 1)) / s).astype(np.float32),
        "wb": (n((K, S)) / np.sqrt(K) / s).astype(np.float32),
        "offs": striped(np.random.permutation(T)[:S]),
        "n1": striped(np.random.permutation(S)),
        "n2": striped(np.random.permutation(S)),
        "cand": striped(np.random.permutation(T)[:C]),
        "cb": striped(np.random.permutation(T)[:C]),
        "n3": striped8(np.stack([np.random.permutation(S)[:W] for _ in range(8)])),
        "n4": striped8(np.stack([np.random.permutation(S)[:W] for _ in range(8)])),
    }


def reference(x_words, x_scales, w1, gs, wb, offs, n1, n2, cand, cb, n3, n4):
    x_cb = unpack_weight(x_words, x_scales)[:, unstriped(cb)]
    b = x_cb.T @ mxq(f64(wb), 0, "e4m3")
    x_cand = unpack_weight(x_words, x_scales)[:, unstriped(cand)]
    xq = unpack_weight(x_words, x_scales)[:, unstriped(offs)]
    y = mxq(f64(w1), 0, "e4m3").T @ xq
    st = np.maximum(y, y[:, unstriped(n1)])
    z = f64(gs) * (np.minimum(st, st[:, unstriped(n2)]))
    a = 0.0625 * ((x_cand.T @ mxq(z, 0, "e4m3")))
    ra = b[np.arange(C)[:, None], runs(n4, C)] - (0.5 * (a[np.arange(C)[:, None], runs(n3, C)]))
    out = a.copy()
    out[np.arange(C)[:, None], runs(n3, C)] = ra
    return out

@@ -1,0 +1,227 @@
+from contextlib import ExitStack
+
+import concourse.mybir as mybir
+
+F32 = mybir.dt.float32
+BF16 = mybir.dt.bfloat16
+I32 = mybir.dt.int32
+U32 = mybir.dt.uint32
+U16 = mybir.dt.uint16
+U8 = mybir.dt.uint8
+FP8X4 = mybir.dt.float8_e4m3fn_x4
+ALU = mybir.AluOpType
+COPY = mybir.ActivationFunctionType.Copy
+
+P = 128
+PACK = 4
+T = 2048
+S = 512
+W = 256
+HALF = 256
+
+FLOPS = 3 * 2 * 512 * 512 * 512
+
+
+def tile_picked_cdswputbhopmn_none_p_kernel(
+    tc, x_words, x_scales, w1, gs, wb, offs, n1, n2, cand, cb, n3, n4, out
+):
+    nc = tc.nc
+    with ExitStack() as ctx:
+        lists = ctx.enter_context(tc.tile_pool(name="lists", bufs=1))
+        keep = ctx.enter_context(tc.tile_pool(name="keep", bufs=1))
+        psum = ctx.enter_context(tc.psum_pool(name="psum", bufs=1))
+
+        def list_tile(name, src):
+            tile = lists.tile([P, src.shape[1]], U16, name=name)
+            nc.sync.dma_start(tile[:], src)
+            return tile
+
+        def sb(name, shape, dtype, tag=None):
+            return keep.tile(shape, dtype, name=name, tag=tag or name, align_bytes=64)
+
+        xs = sb("xs", [P, T], U8)
+        nc.vector.memset(xs[:].bitcast(I32), 0)
+        w1_rows = w1.rearrange("(p j) c -> p j c", j=PACK)
+        w1_raw = [sb("w1_raw%d" % h, [P, PACK, HALF], F32) for h in range(2)]
+        offs_t = list_tile("offs_t", offs)
+        cand_t = list_tile("cand_t", cand)
+        cb_t = list_tile("cb_t", cb)
+        for q in range(4):
+            nc.sync.dma_start(xs[32 * q : 32 * q + 4, :].bitcast(I32), x_scales[0, 4 * q : 4 * q + 4, :].bitcast(I32))
+        nc.sync.dma_start(w1_raw[0][:], w1_rows[:, :, 0:HALF])
+        nc.sync.dma_start(w1_raw[1][:], w1_rows[:, :, HALF:S])
+        xw = sb("xw", [P, T], U32)
+        nc.sync.dma_start(xw[:].bitcast(I32), x_words[0].rearrange("p n t -> p (n t)").bitcast(I32))
+        g = sb("g", [P, PACK], F32)
+        nc.sync.dma_start(g[:], gs.rearrange("(p t) o -> p (t o)", t=PACK))
+        n1_t = list_tile("n1_t", n1)
+        wb_raw = sb("wb_raw", [P, PACK, S], F32)
+        nc.sync.dma_start(wb_raw[:], wb.rearrange("(p j) c -> p j c", j=PACK))
+        n2_t = list_tile("n2_t", n2)
+        n4_t = list_tile("n4_t", n4)
+        n3_t = list_tile("n3_t", n3)
+
+        w1_bf = sb("w1_bf", [P, PACK, P, PACK], BF16)
+        for h in range(2):
+            nc.scalar.copy(
+                w1_bf[:, :, 64 * h : 64 * (h + 1), :].rearrange("p t m j -> p m t j"),
+                w1_raw[h][:].rearrange("p j (m t) -> p m t j", t=PACK),
+            )
+
+        xq_s = sb("xq_s", [P, S], U8)
+        nc.vector.tensor_copy(xq_s[:], xs[:].indirect(offs_t[:]))
+        pick_s = sb("pick_s", [P, 2, S], U8)
+        nc.vector.tensor_copy(pick_s[:, 0, :], xs[:].indirect(cand_t[:]))
+        nc.vector.tensor_copy(pick_s[:, 1, :], xs[:].indirect(cb_t[:]))
+        deal_s = sb("deal_s", [P, 2, S], U8)
+        nc.vector.tensor_copy(
+            deal_s[:].rearrange("p l (t c i) -> p l c t i", t=PACK, i=16),
+            pick_s[:].rearrange("p l (c i t) -> p l c t i", t=PACK, i=16),
+        )
+
+        w1_c = sb("w1_c", [P, S], U32)
+        w1_s = sb("w1_s", [P, S], U8)
+        nc.vector.quantize_mx(out=w1_c[:].bitcast(FP8X4), scales=w1_s[:], in_=w1_bf[:].rearrange("p t m j -> p (t m j)"))
+
+        xq_w = sb("xq_w", [P, S], U32)
+        nc.vector.tensor_copy(xq_w[:], xw[:].indirect(offs_t[:]))
+
+        two = sb("two", [P, PACK], F32)
+        sgn = sb("sgn", [P, PACK], F32)
+        sgn_bf = sb("sgn_bf", [P, PACK], BF16)
+        mag = sb("mag", [P, PACK], F32)
+        nc.gpsimd.tensor_scalar(two[:], g[:], 0.0, 2.0, ALU.is_ge, ALU.mult)
+        nc.gpsimd.tensor_scalar(sgn[:], two[:], 1.0, -1.0, ALU.mult, ALU.add)
+        nc.gpsimd.tensor_scalar(sgn_bf[:], two[:], 1.0, -1.0, ALU.mult, ALU.add)
+        nc.gpsimd.tensor_tensor(mag[:], g[:], sgn[:], ALU.mult)
+
+        def pick_words(name, offsets, tag):
+            picked = sb(name, [P, S], U32, tag=tag)
+            nc.vector.tensor_copy(picked[:], xw[:].indirect(offsets[:]))
+            return picked
+
+        def deal_words(name, picked):
+            dealt = sb(name, [P, S], U32)
+            nc.vector.tensor_copy(
+                dealt[:].bitcast(I32).rearrange("p (t c i) -> p c t i", t=PACK, i=4),
+                picked[:].bitcast(I32).rearrange("p (c i t) -> p c t i", t=PACK, i=4),
+            )
+            return dealt
+
+        st = sb("st", [P, PACK, S], F32)
+        y_banks = []
+        for t in range(PACK):
+            bank = psum.tile([P, S], F32, name="ya%d" % t)
+            cols = slice(P * t, P * (t + 1))
+            nc.tensor.matmul_mx(
+                out=bank[:], lhsT=w1_c[:, cols].bitcast(FP8X4), lhsT_scale=w1_s[:, cols],
+                rhs=xq_w[:].bitcast(FP8X4), rhs_scale=xq_s[:], start=True, stop=True,
+            )
+            y_banks.append(bank)
+
+        ys = {}
+
+        def leave_bank(t):
+            y = sb("y%d" % t, [P, S], F32)
+            if t % 2 == 0:
+                nc.scalar.activation(y[:], y_banks[t][:], COPY, scale=mag[:, t : t + 1])
+            else:
+                nc.vector.tensor_scalar(y[:], y_banks[t][:], mag[:, t : t + 1], None, ALU.mult)
+            ys[t] = y
+
+        def fetch_n1(t):
+            g1 = sb("g1_%d" % t, [P, S], F32)
+            for h in range(2):
+                nc.scalar.activation(g1[:, HALF * h : HALF * (h + 1)], ys[t][:].indirect(n1_t[:, 16 * h : 16 * (h + 1)]), COPY)
+            return g1
+
+        def larger(t, g1):
+            nc.vector.tensor_tensor(st[:, t, :], ys[t][:], g1[:], ALU.max)
+
+        cand_w = deal_words("cand_w", pick_words("cand_p", cand_t, "cand_p"))
+        leave_bank(0)
+        g1_0 = fetch_n1(0)
+        leave_bank(1)
+        g1_1 = fetch_n1(1)
+        larger(0, g1_0)
+        leave_bank(2)
+        g1_2 = fetch_n1(2)
+        leave_bank(3)
+        g1_3 = fetch_n1(3)
+        wb_bf = sb("wb_bf", [P, S, PACK], BF16, tag="xq_w")
+        nc.vector.tensor_copy(
+            wb_bf[:].rearrange("p (c i) j -> p c j i", i=4),
+            wb_raw[:].rearrange("p j (c i) -> p c j i", i=4),
+        )
+        larger(1, g1_1)
+        cb_p = pick_words("cb_p", cb_t, "w1_c")
+        larger(2, g1_2)
+        larger(3, g1_3)
+        cb_w = deal_words("cb_w", cb_p)
+        wb_c = sb("wb_c", [P, S], U32)
+        wb_s = sb("wb_s", [P, S], U8)
+        nc.vector.quantize_mx(out=wb_c[:].bitcast(FP8X4), scales=wb_s[:], in_=wb_bf[:].rearrange("p c j -> p (c j)"))
+
+        b_banks = []
+        for t in range(PACK):
+            bank = psum.tile([P, S], F32, name="b%d" % t)
+            cols = slice(P * t, P * (t + 1))
+            nc.tensor.matmul_mx(
+                out=bank[:], lhsT=cb_w[:, cols].bitcast(FP8X4), lhsT_scale=deal_s[:, 1, cols],
+                rhs=wb_c[:].bitcast(FP8X4), rhs_scale=wb_s[:], start=True, stop=True,
+            )
+            b_banks.append(bank)
+
+        a_banks = [psum.tile([P, S], F32, name="ya%d" % t) for t in range(PACK)]
+        for h in range(2):
+            cols = slice(HALF * h, HALF * (h + 1))
+            g2 = sb("g2_%d" % h, [P, PACK, HALF], F32)
+            for t in range(PACK):
+                looked_up = st[:, t, :].indirect(n2_t[:, 16 * h : 16 * (h + 1)])
+                nc.scalar.activation(g2[:, t, :], looked_up, COPY)
+            m_bf = sb("m_bf%d" % h, [P, HALF, PACK], BF16)
+            nc.vector.tensor_tensor(
+                m_bf[:].rearrange("p (c i) t -> p c t i", i=4),
+                st[:, :, cols].rearrange("p t (c i) -> p c t i", i=4),
+                g2[:].rearrange("p t (c i) -> p c t i", i=4),
+                ALU.min,
+            )
+            z_bf = sb("z_bf%d" % h, [P, HALF, PACK], BF16)
+            nc.vector.tensor_tensor(z_bf[:], m_bf[:], sgn_bf[:].unsqueeze(1).to_broadcast([P, HALF, PACK]), ALU.mult)
+            z_c = sb("z_c%d" % h, [P, HALF], U32)
+            z_s = sb("z_s%d" % h, [P, HALF], U8)
+            nc.vector.quantize_mx(out=z_c[:].bitcast(FP8X4), scales=z_s[:], in_=z_bf[:].rearrange("p c t -> p (c t)"))
+            for t in range(PACK):
+                rows = slice(P * t, P * (t + 1))
+                nc.tensor.matmul_mx(
+                    out=a_banks[t][:, cols], lhsT=cand_w[:, rows].bitcast(FP8X4), lhsT_scale=deal_s[:, 0, rows],
+                    rhs=z_c[:].bitcast(FP8X4), rhs_scale=z_s[:], start=True, stop=True,
+                )
+
+        out_rows = out.rearrange("(p t) c -> t p c", t=PACK)
+        b_tags = ["g2_0", "m_bf0", "z_bf1", "z_s1"]
+        gb_tags = ["gb0", "gb1", "z_c1", "gb3"]
+        bs = []
+        for t in range(PACK):
+            b = sb("bs%d" % t, [P, S], F32, tag=b_tags[t])
+            if t < 2:
+                nc.scalar.copy(b[:], b_banks[t][:])
+            else:
+                nc.vector.tensor_copy(b[:], b_banks[t][:])
+            bs.append(b)
+
+        def fetch_b(t):
+            gb = sb("gb%d" % t, [P, W], F32, tag=gb_tags[t])
+            nc.scalar.activation(gb[:], bs[t][:].indirect(n4_t[:]), COPY)
+            return gb
+
+        gbs = [fetch_b(0), fetch_b(1)]
+        for t in range(PACK):
+            if t >= 2:
+                gbs.append(fetch_b(t))
+            a = sb("a%d" % t, [P, S], F32)
+            nc.scalar.activation(a[:], a_banks[t][:], COPY, scale=0.0625)
+            ga = sb("ga%d" % t, [P, W], F32)
+            nc.scalar.activation(ga[:], a[:].indirect(n3_t[:]), COPY, scale=-0.5)
+            nc.vector.tensor_tensor(a[:].indirect(n3_t[:]), gbs[t][:], ga[:], ALU.add)
+            nc.sync.dma_start(out_rows[t], a[:])

@@ -18,6 +18,7 @@ T = 2048
 S = 512
 W = 256
 HALF = 256
+SPARE = 32
 
 FLOPS = 3 * 2 * 512 * 512 * 512
 
@@ -29,6 +30,7 @@ def tile_picked_cdswputbhopmn_none_p_kernel(
     with ExitStack() as ctx:
         lists = ctx.enter_context(tc.tile_pool(name="lists", bufs=1))
         keep = ctx.enter_context(tc.tile_pool(name="keep", bufs=1))
+        shared = ctx.enter_context(tc.tile_pool(name="shared", bufs=1))
         psum = ctx.enter_context(tc.psum_pool(name="psum", bufs=1))
 
         def list_tile(name, src):
@@ -40,14 +42,14 @@ def tile_picked_cdswputbhopmn_none_p_kernel(
             return keep.tile(shape, dtype, name=name, tag=tag or name, align_bytes=64)
 
         xs = sb("xs", [P, T], U8)
-        nc.vector.memset(xs[:].bitcast(I32), 0)
+        nc.gpsimd.memset(xs[:].bitcast(I32), 0)
         w1_rows = w1.rearrange("(p j) c -> p j c", j=PACK)
         w1_raw = [sb("w1_raw%d" % h, [P, PACK, HALF], F32) for h in range(2)]
         offs_t = list_tile("offs_t", offs)
-        cand_t = list_tile("cand_t", cand)
-        cb_t = list_tile("cb_t", cb)
         for q in range(4):
             nc.sync.dma_start(xs[32 * q : 32 * q + 4, :].bitcast(I32), x_scales[0, 4 * q : 4 * q + 4, :].bitcast(I32))
+        cand_t = list_tile("cand_t", cand)
+        cb_t = list_tile("cb_t", cb)
         nc.sync.dma_start(w1_raw[0][:], w1_rows[:, :, 0:HALF])
         nc.sync.dma_start(w1_raw[1][:], w1_rows[:, :, HALF:S])
         xw = sb("xw", [P, T], U32)
@@ -61,7 +63,7 @@ def tile_picked_cdswputbhopmn_none_p_kernel(
         n4_t = list_tile("n4_t", n4)
         n3_t = list_tile("n3_t", n3)
 
-        w1_bf = sb("w1_bf", [P, PACK, P, PACK], BF16)
+        w1_bf = shared.tile([P, PACK, P, PACK], BF16, name="w1_bf", align_bytes=64, offset=1024)
         for h in range(2):
             nc.scalar.copy(
                 w1_bf[:, :, 64 * h : 64 * (h + 1), :].rearrange("p t m j -> p m t j"),
@@ -73,18 +75,14 @@ def tile_picked_cdswputbhopmn_none_p_kernel(
         pick_s = sb("pick_s", [P, 2, S], U8)
         nc.vector.tensor_copy(pick_s[:, 0, :], xs[:].indirect(cand_t[:]))
         nc.vector.tensor_copy(pick_s[:, 1, :], xs[:].indirect(cb_t[:]))
-        deal_s = sb("deal_s", [P, 2, S], U8)
-        nc.vector.tensor_copy(
-            deal_s[:].rearrange("p l (t c i) -> p l c t i", t=PACK, i=16),
-            pick_s[:].rearrange("p l (c i t) -> p l c t i", t=PACK, i=16),
-        )
 
         w1_c = sb("w1_c", [P, S], U32)
         w1_s = sb("w1_s", [P, S], U8)
         nc.vector.quantize_mx(out=w1_c[:].bitcast(FP8X4), scales=w1_s[:], in_=w1_bf[:].rearrange("p t m j -> p (t m j)"))
 
-        xq_w = sb("xq_w", [P, S], U32)
-        nc.vector.tensor_copy(xq_w[:], xw[:].indirect(offs_t[:]))
+        xq_w = shared.tile([P, S], U32, name="xq_w", align_bytes=64, offset=0)
+        for h in range(2):
+            nc.vector.tensor_copy(xq_w[:, HALF * h : HALF * (h + 1)], xw[:].indirect(offs_t[:, 16 * h : 16 * (h + 1)]))
 
         two = sb("two", [P, PACK], F32)
         sgn = sb("sgn", [P, PACK], F32)
@@ -95,133 +93,131 @@ def tile_picked_cdswputbhopmn_none_p_kernel(
         nc.gpsimd.tensor_scalar(sgn_bf[:], two[:], 1.0, -1.0, ALU.mult, ALU.add)
         nc.gpsimd.tensor_tensor(mag[:], g[:], sgn[:], ALU.mult)
 
-        def pick_words(name, offsets, tag):
-            picked = sb(name, [P, S], U32, tag=tag)
-            nc.vector.tensor_copy(picked[:], xw[:].indirect(offsets[:]))
-            return picked
-
-        def deal_words(name, picked):
-            dealt = sb(name, [P, S], U32)
-            nc.vector.tensor_copy(
-                dealt[:].bitcast(I32).rearrange("p (t c i) -> p c t i", t=PACK, i=4),
-                picked[:].bitcast(I32).rearrange("p (c i t) -> p c t i", t=PACK, i=4),
-            )
-            return dealt
-
         st = sb("st", [P, PACK, S], F32)
-        y_banks = []
-        for t in range(PACK):
-            bank = psum.tile([P, S], F32, name="ya%d" % t)
-            cols = slice(P * t, P * (t + 1))
+
+        def project(t, bank, cols):
+            rows = slice(P * t, P * (t + 1))
             nc.tensor.matmul_mx(
-                out=bank[:], lhsT=w1_c[:, cols].bitcast(FP8X4), lhsT_scale=w1_s[:, cols],
-                rhs=xq_w[:].bitcast(FP8X4), rhs_scale=xq_s[:], start=True, stop=True,
+                out=bank[:, cols], lhsT=w1_c[:, rows].bitcast(FP8X4), lhsT_scale=w1_s[:, rows],
+                rhs=xq_w[:, cols].bitcast(FP8X4), rhs_scale=xq_s[:, cols], start=True, stop=True,
             )
-            y_banks.append(bank)
 
-        ys = {}
-
-        def leave_bank(t):
-            y = sb("y%d" % t, [P, S], F32)
-            if t % 2 == 0:
-                nc.scalar.activation(y[:], y_banks[t][:], COPY, scale=mag[:, t : t + 1])
-            else:
-                nc.vector.tensor_scalar(y[:], y_banks[t][:], mag[:, t : t + 1], None, ALU.mult)
-            ys[t] = y
-
-        def fetch_n1(t):
+        ys = []
+        g1s = []
+        for t in range(PACK):
+            y = sb("y%d" % t, [P, S + SPARE], F32)
+            nc.gpsimd.memset(y[:, S : S + SPARE], 0.0)
+            pieces = [("b3", slice(0, HALF)), ("ya0", slice(HALF, S))] if t == 0 else [("ya%d" % t, slice(0, S))]
+            for tag, cols in pieces:
+                bank = psum.tile([P, S], F32, name=tag)
+                project(t, bank, cols)
+                nc.scalar.activation(y[:, cols], bank[:, cols], COPY, scale=mag[:, t : t + 1])
             g1 = sb("g1_%d" % t, [P, S], F32)
-            for h in range(2):
-                nc.scalar.activation(g1[:, HALF * h : HALF * (h + 1)], ys[t][:].indirect(n1_t[:, 16 * h : 16 * (h + 1)]), COPY)
-            return g1
+            if t % 2 == 0:
+                nc.scalar.activation(g1[:], y[:].indirect(n1_t[:]), COPY)
+            else:
+                nc.scalar.activation(g1[:, 0:HALF], y[:].indirect(n1_t[:, 0:16]), COPY)
+            ys.append(y)
+            g1s.append(g1)
 
-        def larger(t, g1):
-            nc.vector.tensor_tensor(st[:, t, :], ys[t][:], g1[:], ALU.max)
+        def larger(t):
+            nc.vector.tensor_tensor(st[:, t, :], ys[t][:, 0:S], g1s[t][:], ALU.max)
 
-        cand_w = deal_words("cand_w", pick_words("cand_p", cand_t, "cand_p"))
-        leave_bank(0)
-        g1_0 = fetch_n1(0)
-        leave_bank(1)
-        g1_1 = fetch_n1(1)
-        larger(0, g1_0)
-        leave_bank(2)
-        g1_2 = fetch_n1(2)
-        leave_bank(3)
-        g1_3 = fetch_n1(3)
-        wb_bf = sb("wb_bf", [P, S, PACK], BF16, tag="xq_w")
+        pick_w = shared.tile([P, 2, S], U32, name="pick_w", align_bytes=64, offset=2048)
+        nc.vector.tensor_copy(pick_w[:, 0, :], xw[:].indirect(cand_t[:]))
+        nc.vector.tensor_copy(pick_w[:, 1, :], xw[:].indirect(cb_t[:]))
+        deal_w = sb("deal_w", [P, 2, S], U32)
+        wb_bf = sb("wb_bf", [P, S, PACK], BF16)
+        for c in range(4):
+            cols = slice(P * c, P * (c + 1))
+            nc.gpsimd.tensor_scalar(wb_bf[:, cols, :], wb_raw[:, :, cols].rearrange("p j c -> p c j"), 1.0, 0.0, ALU.mult, ALU.add)
+        deal_s = sb("deal_s", [P, 2, S], U8, tag="xq_s")
         nc.vector.tensor_copy(
-            wb_bf[:].rearrange("p (c i) j -> p c j i", i=4),
-            wb_raw[:].rearrange("p j (c i) -> p c j i", i=4),
+            deal_s[:].rearrange("p l (t c i) -> p l c t i", t=PACK, i=16),
+            pick_s[:].rearrange("p l (c i t) -> p l c t i", t=PACK, i=16),
         )
-        larger(1, g1_1)
-        cb_p = pick_words("cb_p", cb_t, "w1_c")
-        larger(2, g1_2)
-        larger(3, g1_3)
-        cb_w = deal_words("cb_w", cb_p)
+        nc.vector.tensor_copy(
+            deal_w[:].bitcast(I32).rearrange("p l (t c i) -> p l c t i", t=PACK, i=4),
+            pick_w[:].bitcast(I32).rearrange("p l (c i t) -> p l c t i", t=PACK, i=4),
+        )
+        larger(0)
+        nc.vector.tensor_copy(g1s[1][:, HALF:S], ys[1][:].indirect(n1_t[:, 16:32]))
         wb_c = sb("wb_c", [P, S], U32)
         wb_s = sb("wb_s", [P, S], U8)
         nc.vector.quantize_mx(out=wb_c[:].bitcast(FP8X4), scales=wb_s[:], in_=wb_bf[:].rearrange("p c j -> p (c j)"))
+        larger(1)
+        larger(2)
+        nc.vector.tensor_copy(g1s[3][:, HALF:S], ys[3][:].indirect(n1_t[:, 16:32]))
+        larger(3)
 
         b_banks = []
         for t in range(PACK):
             bank = psum.tile([P, S], F32, name="b%d" % t)
             cols = slice(P * t, P * (t + 1))
             nc.tensor.matmul_mx(
-                out=bank[:], lhsT=cb_w[:, cols].bitcast(FP8X4), lhsT_scale=deal_s[:, 1, cols],
+                out=bank[:], lhsT=deal_w[:, 1, cols].bitcast(FP8X4), lhsT_scale=deal_s[:, 1, cols],
                 rhs=wb_c[:].bitcast(FP8X4), rhs_scale=wb_s[:], start=True, stop=True,
             )
             b_banks.append(bank)
 
+        def fetch_b(t):
+            if t < 2:
+                b = sb("bs%d" % t, [P, S], F32, tag="g2_%d" % t)
+                nc.scalar.copy(b[:], b_banks[t][:])
+                gb = sb("gb%d" % t, [P, W], F32)
+            else:
+                b = shared.tile([P, S], F32, name="bs%d" % t, align_bytes=64, offset=2048 * t)
+                nc.vector.tensor_copy(b[:], b_banks[t][:])
+                gb = sb("gb%d" % t, [P, W], F32, tag=("z_c1", "z_s1")[t - 2])
+            nc.scalar.activation(gb[:], b[:].indirect(n4_t[:]), COPY)
+            return gb
+
+        gbs = []
         a_banks = [psum.tile([P, S], F32, name="ya%d" % t) for t in range(PACK)]
         for h in range(2):
             cols = slice(HALF * h, HALF * (h + 1))
             g2 = sb("g2_%d" % h, [P, PACK, HALF], F32)
             for t in range(PACK):
                 looked_up = st[:, t, :].indirect(n2_t[:, 16 * h : 16 * (h + 1)])
-                nc.scalar.activation(g2[:, t, :], looked_up, COPY)
-            m_bf = sb("m_bf%d" % h, [P, HALF, PACK], BF16)
+                if h == 0 and t == 3:
+                    nc.vector.tensor_copy(g2[:, t, :], looked_up)
+                else:
+                    nc.scalar.activation(g2[:, t, :], looked_up, COPY)
+            m_bf = sb("m_bf%d" % h, [P, HALF, PACK], BF16, tag="m_bf")
             nc.vector.tensor_tensor(
                 m_bf[:].rearrange("p (c i) t -> p c t i", i=4),
                 st[:, :, cols].rearrange("p t (c i) -> p c t i", i=4),
                 g2[:].rearrange("p t (c i) -> p c t i", i=4),
                 ALU.min,
             )
-            z_bf = sb("z_bf%d" % h, [P, HALF, PACK], BF16)
+            gbs.append(fetch_b(h))
+            z_bf = shared.tile([P, HALF, PACK], BF16, name="z_bf%d" % h, align_bytes=64, offset=(8192, 5120)[h])
             nc.vector.tensor_tensor(z_bf[:], m_bf[:], sgn_bf[:].unsqueeze(1).to_broadcast([P, HALF, PACK]), ALU.mult)
             z_c = sb("z_c%d" % h, [P, HALF], U32)
             z_s = sb("z_s%d" % h, [P, HALF], U8)
             nc.vector.quantize_mx(out=z_c[:].bitcast(FP8X4), scales=z_s[:], in_=z_bf[:].rearrange("p c t -> p (c t)"))
             for t in range(PACK):
                 rows = slice(P * t, P * (t + 1))
+                bank = psum.tile([P, S], F32, name="b0") if (h, t) == (0, 0) else a_banks[t]
+                if (h, t) == (0, 0):
+                    a0_first = bank
                 nc.tensor.matmul_mx(
-                    out=a_banks[t][:, cols], lhsT=cand_w[:, rows].bitcast(FP8X4), lhsT_scale=deal_s[:, 0, rows],
+                    out=bank[:, cols], lhsT=deal_w[:, 0, rows].bitcast(FP8X4), lhsT_scale=deal_s[:, 0, rows],
                     rhs=z_c[:].bitcast(FP8X4), rhs_scale=z_s[:], start=True, stop=True,
                 )
 
         out_rows = out.rearrange("(p t) c -> t p c", t=PACK)
-        b_tags = ["g2_0", "m_bf0", "z_bf1", "z_s1"]
-        gb_tags = ["gb0", "gb1", "z_c1", "gb3"]
-        bs = []
-        for t in range(PACK):
-            b = sb("bs%d" % t, [P, S], F32, tag=b_tags[t])
-            if t < 2:
-                nc.scalar.copy(b[:], b_banks[t][:])
-            else:
-                nc.vector.tensor_copy(b[:], b_banks[t][:])
-            bs.append(b)
-
-        def fetch_b(t):
-            gb = sb("gb%d" % t, [P, W], F32, tag=gb_tags[t])
-            nc.scalar.activation(gb[:], bs[t][:].indirect(n4_t[:]), COPY)
-            return gb
-
-        gbs = [fetch_b(0), fetch_b(1)]
         for t in range(PACK):
             if t >= 2:
                 gbs.append(fetch_b(t))
             a = sb("a%d" % t, [P, S], F32)
-            nc.scalar.activation(a[:], a_banks[t][:], COPY, scale=0.0625)
             ga = sb("ga%d" % t, [P, W], F32)
-            nc.scalar.activation(ga[:], a[:].indirect(n3_t[:]), COPY, scale=-0.5)
+            if t == 0:
+                nc.scalar.activation(a[:, 0:HALF], a0_first[:, 0:HALF], COPY, scale=0.0625)
+                nc.scalar.activation(a[:, HALF:S], a_banks[t][:, HALF:S], COPY, scale=0.0625)
+                nc.vector.tensor_scalar(ga[:], a[:].indirect(n3_t[:]), -0.5, 0.0, ALU.mult, ALU.add)
+            else:
+                nc.scalar.activation(a[:], a_banks[t][:], COPY, scale=0.0625)
+                nc.scalar.activation(ga[:], a[:].indirect(n3_t[:]), COPY, scale=-0.5)
             nc.vector.tensor_tensor(a[:].indirect(n3_t[:]), gbs[t][:], ga[:], ALU.add)
             nc.sync.dma_start(out_rows[t], a[:])

@@ -19,6 +19,7 @@ S = 512
 W = 256
 HALF = 256
 SPARE = 32
+W1_SPLIT = 80
 
 FLOPS = 3 * 2 * 512 * 512 * 512
 
@@ -44,14 +45,13 @@ def tile_picked_cdswputbhopmn_none_p_kernel(
         xs = sb("xs", [P, T], U8)
         nc.gpsimd.memset(xs[:].bitcast(I32), 0)
         w1_rows = w1.rearrange("(p j) c -> p j c", j=PACK)
-        w1_raw = [sb("w1_raw%d" % h, [P, PACK, HALF], F32) for h in range(2)]
+        w1_raw = sb("w1_raw", [P, PACK, S], F32)
         offs_t = list_tile("offs_t", offs)
         for q in range(4):
             nc.sync.dma_start(xs[32 * q : 32 * q + 4, :].bitcast(I32), x_scales[0, 4 * q : 4 * q + 4, :].bitcast(I32))
         cand_t = list_tile("cand_t", cand)
+        nc.sync.dma_start(w1_raw[:], w1_rows)
         cb_t = list_tile("cb_t", cb)
-        nc.sync.dma_start(w1_raw[0][:], w1_rows[:, :, 0:HALF])
-        nc.sync.dma_start(w1_raw[1][:], w1_rows[:, :, HALF:S])
         xw = sb("xw", [P, T], U32)
         nc.sync.dma_start(xw[:].bitcast(I32), x_words[0].rearrange("p n t -> p (n t)").bitcast(I32))
         g = sb("g", [P, PACK], F32)
@@ -63,12 +63,11 @@ def tile_picked_cdswputbhopmn_none_p_kernel(
         n4_t = list_tile("n4_t", n4)
         n3_t = list_tile("n3_t", n3)
 
-        w1_bf = shared.tile([P, PACK, P, PACK], BF16, name="w1_bf", align_bytes=64, offset=1024)
-        for h in range(2):
-            nc.scalar.copy(
-                w1_bf[:, :, 64 * h : 64 * (h + 1), :].rearrange("p t m j -> p m t j"),
-                w1_raw[h][:].rearrange("p j (m t) -> p m t j", t=PACK),
-            )
+        w1_bf = shared.tile([P, PACK, P, PACK], BF16, name="w1_bf", align_bytes=64, offset=5632)
+        w1_src = w1_raw[:].rearrange("p j (m t) -> p m t j", t=PACK)
+        w1_dst = w1_bf[:].rearrange("p t m j -> p m t j")
+        nc.scalar.copy(w1_dst[:, 0:W1_SPLIT], w1_src[:, 0:W1_SPLIT])
+        nc.gpsimd.tensor_scalar(w1_dst[:, W1_SPLIT:P], w1_src[:, W1_SPLIT:P], 1.0, 0.0, ALU.mult, ALU.add)
 
         xq_s = sb("xq_s", [P, S], U8)
         nc.vector.tensor_copy(xq_s[:], xs[:].indirect(offs_t[:]))
@@ -80,7 +79,7 @@ def tile_picked_cdswputbhopmn_none_p_kernel(
         w1_s = sb("w1_s", [P, S], U8)
         nc.vector.quantize_mx(out=w1_c[:].bitcast(FP8X4), scales=w1_s[:], in_=w1_bf[:].rearrange("p t m j -> p (t m j)"))
 
-        xq_w = shared.tile([P, S], U32, name="xq_w", align_bytes=64, offset=0)
+        xq_w = shared.tile([P, S], U32, name="xq_w", align_bytes=64, offset=4096)
         for h in range(2):
             nc.vector.tensor_copy(xq_w[:, HALF * h : HALF * (h + 1)], xw[:].indirect(offs_t[:, 16 * h : 16 * (h + 1)]))
 
@@ -123,25 +122,25 @@ def tile_picked_cdswputbhopmn_none_p_kernel(
         def larger(t):
             nc.vector.tensor_tensor(st[:, t, :], ys[t][:, 0:S], g1s[t][:], ALU.max)
 
-        pick_w = shared.tile([P, 2, S], U32, name="pick_w", align_bytes=64, offset=2048)
-        nc.vector.tensor_copy(pick_w[:, 0, :], xw[:].indirect(cand_t[:]))
-        nc.vector.tensor_copy(pick_w[:, 1, :], xw[:].indirect(cb_t[:]))
-        deal_w = sb("deal_w", [P, 2, S], U32)
-        wb_bf = sb("wb_bf", [P, S, PACK], BF16)
-        for c in range(4):
-            cols = slice(P * c, P * (c + 1))
-            nc.gpsimd.tensor_scalar(wb_bf[:, cols, :], wb_raw[:, :, cols].rearrange("p j c -> p c j"), 1.0, 0.0, ALU.mult, ALU.add)
-        deal_s = sb("deal_s", [P, 2, S], U8, tag="xq_s")
+        deal_s = shared.tile([P, 2, S], U8, name="deal_s", align_bytes=64, offset=6144)
         nc.vector.tensor_copy(
             deal_s[:].rearrange("p l (t c i) -> p l c t i", t=PACK, i=16),
             pick_s[:].rearrange("p l (c i t) -> p l c t i", t=PACK, i=16),
         )
+        pick_w = shared.tile([P, 2, S], U32, name="pick_w", align_bytes=64, offset=7168)
+        nc.vector.tensor_copy(pick_w[:, 0, :], xw[:].indirect(cand_t[:]))
+        nc.vector.tensor_copy(pick_w[:, 1, :], xw[:].indirect(cb_t[:]))
+        nc.vector.tensor_copy(g1s[1][:, HALF:S], ys[1][:].indirect(n1_t[:, 16:32]))
+        larger(0)
+        deal_w = shared.tile([P, 2, S], U32, name="deal_w", align_bytes=64, offset=1024)
+        wb_bf = sb("wb_bf", [P, S, PACK], BF16)
+        for c in range(4):
+            cols = slice(P * c, P * (c + 1))
+            nc.gpsimd.tensor_scalar(wb_bf[:, cols, :], wb_raw[:, :, cols].rearrange("p j c -> p c j"), 1.0, 0.0, ALU.mult, ALU.add)
         nc.vector.tensor_copy(
             deal_w[:].bitcast(I32).rearrange("p l (t c i) -> p l c t i", t=PACK, i=4),
             pick_w[:].bitcast(I32).rearrange("p l (c i t) -> p l c t i", t=PACK, i=4),
         )
-        larger(0)
-        nc.vector.tensor_copy(g1s[1][:, HALF:S], ys[1][:].indirect(n1_t[:, 16:32]))
         wb_c = sb("wb_c", [P, S], U32)
         wb_s = sb("wb_s", [P, S], U8)
         nc.vector.quantize_mx(out=wb_c[:].bitcast(FP8X4), scales=wb_s[:], in_=wb_bf[:].rearrange("p c j -> p (c j)"))
@@ -166,11 +165,21 @@ def tile_picked_cdswputbhopmn_none_p_kernel(
                 nc.scalar.copy(b[:], b_banks[t][:])
                 gb = sb("gb%d" % t, [P, W], F32)
             else:
-                b = shared.tile([P, S], F32, name="bs%d" % t, align_bytes=64, offset=2048 * t)
+                b = shared.tile([P, S], F32, name="bs%d" % t, align_bytes=64, offset=8192 + 2048 * t)
                 nc.vector.tensor_copy(b[:], b_banks[t][:])
-                gb = sb("gb%d" % t, [P, W], F32, tag=("z_c1", "z_s1")[t - 2])
+                gb = sb("gb%d" % t, [P, W], F32, tag=("z_c", "z_s")[t - 2])
             nc.scalar.activation(gb[:], b[:].indirect(n4_t[:]), COPY)
             return gb
+
+        z_c = sb("z_c", [P, S], U32)
+        z_s = sb("z_s", [P, S], U8)
+
+        def score(t, bank, cols):
+            rows = slice(P * t, P * (t + 1))
+            nc.tensor.matmul_mx(
+                out=bank[:, cols], lhsT=deal_w[:, 0, rows].bitcast(FP8X4), lhsT_scale=deal_s[:, 0, rows],
+                rhs=z_c[:, cols].bitcast(FP8X4), rhs_scale=z_s[:, cols], start=True, stop=True,
+            )
 
         gbs = []
         a_banks = [psum.tile([P, S], F32, name="ya%d" % t) for t in range(PACK)]
@@ -191,20 +200,14 @@ def tile_picked_cdswputbhopmn_none_p_kernel(
                 ALU.min,
             )
             gbs.append(fetch_b(h))
-            z_bf = shared.tile([P, HALF, PACK], BF16, name="z_bf%d" % h, align_bytes=64, offset=(8192, 5120)[h])
+            z_bf = shared.tile([P, HALF, PACK], BF16, name="z_bf%d" % h, align_bytes=64, offset=(16384, 13312)[h])
             nc.vector.tensor_tensor(z_bf[:], m_bf[:], sgn_bf[:].unsqueeze(1).to_broadcast([P, HALF, PACK]), ALU.mult)
-            z_c = sb("z_c%d" % h, [P, HALF], U32)
-            z_s = sb("z_s%d" % h, [P, HALF], U8)
-            nc.vector.quantize_mx(out=z_c[:].bitcast(FP8X4), scales=z_s[:], in_=z_bf[:].rearrange("p c t -> p (c t)"))
-            for t in range(PACK):
-                rows = slice(P * t, P * (t + 1))
-                bank = psum.tile([P, S], F32, name="b0") if (h, t) == (0, 0) else a_banks[t]
-                if (h, t) == (0, 0):
-                    a0_first = bank
-                nc.tensor.matmul_mx(
-                    out=bank[:, cols], lhsT=deal_w[:, 0, rows].bitcast(FP8X4), lhsT_scale=deal_s[:, 0, rows],
-                    rhs=z_c[:].bitcast(FP8X4), rhs_scale=z_s[:], start=True, stop=True,
-                )
+            nc.vector.quantize_mx(out=z_c[:, cols].bitcast(FP8X4), scales=z_s[:, cols], in_=z_bf[:].rearrange("p c t -> p (c t)"))
+            if h == 0:
+                a0_first = psum.tile([P, S], F32, name="b0")
+            score(0, a0_first if h == 0 else a_banks[0], cols)
+        for t in range(1, PACK):
+            score(t, a_banks[t], slice(0, S))
 
         out_rows = out.rearrange("(p t) c -> t p c", t=PACK)
         for t in range(PACK):

@@ -19,7 +19,6 @@ S = 512
 W = 256
 HALF = 256
 SPARE = 32
-W1_SPLIT = 80
 
 FLOPS = 3 * 2 * 512 * 512 * 512
 
@@ -45,13 +44,14 @@ def tile_picked_cdswputbhopmn_none_p_kernel(
         xs = sb("xs", [P, T], U8)
         nc.gpsimd.memset(xs[:].bitcast(I32), 0)
         w1_rows = w1.rearrange("(p j) c -> p j c", j=PACK)
-        w1_raw = sb("w1_raw", [P, PACK, S], F32)
+        w1_raw = [sb("w1_raw%d" % h, [P, PACK, HALF], F32) for h in range(2)]
         offs_t = list_tile("offs_t", offs)
         for q in range(4):
             nc.sync.dma_start(xs[32 * q : 32 * q + 4, :].bitcast(I32), x_scales[0, 4 * q : 4 * q + 4, :].bitcast(I32))
         cand_t = list_tile("cand_t", cand)
-        nc.sync.dma_start(w1_raw[:], w1_rows)
         cb_t = list_tile("cb_t", cb)
+        nc.sync.dma_start(w1_raw[0][:], w1_rows[:, :, 0:HALF])
+        nc.sync.dma_start(w1_raw[1][:], w1_rows[:, :, HALF:S])
         xw = sb("xw", [P, T], U32)
         nc.sync.dma_start(xw[:].bitcast(I32), x_words[0].rearrange("p n t -> p (n t)").bitcast(I32))
         g = sb("g", [P, PACK], F32)
@@ -64,10 +64,11 @@ def tile_picked_cdswputbhopmn_none_p_kernel(
         n3_t = list_tile("n3_t", n3)
 
         w1_bf = shared.tile([P, PACK, P, PACK], BF16, name="w1_bf", align_bytes=64, offset=5632)
-        w1_src = w1_raw[:].rearrange("p j (m t) -> p m t j", t=PACK)
-        w1_dst = w1_bf[:].rearrange("p t m j -> p m t j")
-        nc.scalar.copy(w1_dst[:, 0:W1_SPLIT], w1_src[:, 0:W1_SPLIT])
-        nc.gpsimd.tensor_scalar(w1_dst[:, W1_SPLIT:P], w1_src[:, W1_SPLIT:P], 1.0, 0.0, ALU.mult, ALU.add)
+        for h in range(2):
+            nc.scalar.copy(
+                w1_bf[:, :, 64 * h : 64 * (h + 1), :].rearrange("p t m j -> p m t j"),
+                w1_raw[h][:].rearrange("p j (m t) -> p m t j", t=PACK),
+            )
 
         xq_s = sb("xq_s", [P, S], U8)
         nc.vector.tensor_copy(xq_s[:], xs[:].indirect(offs_t[:]))
@@ -112,10 +113,10 @@ def tile_picked_cdswputbhopmn_none_p_kernel(
                 project(t, bank, cols)
                 nc.scalar.activation(y[:, cols], bank[:, cols], COPY, scale=mag[:, t : t + 1])
             g1 = sb("g1_%d" % t, [P, S], F32)
-            if t % 2 == 0:
+            if t < 3:
                 nc.scalar.activation(g1[:], y[:].indirect(n1_t[:]), COPY)
             else:
-                nc.scalar.activation(g1[:, 0:HALF], y[:].indirect(n1_t[:, 0:16]), COPY)
+                nc.scalar.activation(g1[:, 0:384], y[:].indirect(n1_t[:, 0:24]), COPY)
             ys.append(y)
             g1s.append(g1)
 
@@ -130,23 +131,23 @@ def tile_picked_cdswputbhopmn_none_p_kernel(
         pick_w = shared.tile([P, 2, S], U32, name="pick_w", align_bytes=64, offset=7168)
         nc.vector.tensor_copy(pick_w[:, 0, :], xw[:].indirect(cand_t[:]))
         nc.vector.tensor_copy(pick_w[:, 1, :], xw[:].indirect(cb_t[:]))
-        nc.vector.tensor_copy(g1s[1][:, HALF:S], ys[1][:].indirect(n1_t[:, 16:32]))
-        larger(0)
-        deal_w = shared.tile([P, 2, S], U32, name="deal_w", align_bytes=64, offset=1024)
         wb_bf = sb("wb_bf", [P, S, PACK], BF16)
-        for c in range(4):
-            cols = slice(P * c, P * (c + 1))
-            nc.gpsimd.tensor_scalar(wb_bf[:, cols, :], wb_raw[:, :, cols].rearrange("p j c -> p c j"), 1.0, 0.0, ALU.mult, ALU.add)
+        nc.vector.tensor_copy(
+            wb_bf[:].rearrange("p (c i) j -> p c j i", i=4),
+            wb_raw[:].rearrange("p j (c i) -> p c j i", i=4),
+        )
+        deal_w = sb("deal_w", [P, 2, S], U32)
         nc.vector.tensor_copy(
             deal_w[:].bitcast(I32).rearrange("p l (t c i) -> p l c t i", t=PACK, i=4),
             pick_w[:].bitcast(I32).rearrange("p l (c i t) -> p l c t i", t=PACK, i=4),
         )
+        larger(0)
         wb_c = sb("wb_c", [P, S], U32)
         wb_s = sb("wb_s", [P, S], U8)
         nc.vector.quantize_mx(out=wb_c[:].bitcast(FP8X4), scales=wb_s[:], in_=wb_bf[:].rearrange("p c j -> p (c j)"))
         larger(1)
         larger(2)
-        nc.vector.tensor_copy(g1s[3][:, HALF:S], ys[3][:].indirect(n1_t[:, 16:32]))
+        nc.vector.tensor_copy(g1s[3][:, 384:S], ys[3][:].indirect(n1_t[:, 24:32]))
         larger(3)
 
         b_banks = []
@@ -160,14 +161,14 @@ def tile_picked_cdswputbhopmn_none_p_kernel(
             b_banks.append(bank)
 
         def fetch_b(t):
-            if t < 2:
-                b = sb("bs%d" % t, [P, S], F32, tag="g2_%d" % t)
+            if t < 3:
+                b = sb("bs%d" % t, [P, S], F32, tag="g2_%d" % (t % 2))
                 nc.scalar.copy(b[:], b_banks[t][:])
-                gb = sb("gb%d" % t, [P, W], F32)
+                gb = sb("gb%d" % t, [P, W], F32, tag="z_s" if t == 2 else None)
             else:
-                b = shared.tile([P, S], F32, name="bs%d" % t, align_bytes=64, offset=8192 + 2048 * t)
+                b = sb("bs%d" % t, [P, S], F32, tag="z_bf1")
                 nc.vector.tensor_copy(b[:], b_banks[t][:])
-                gb = sb("gb%d" % t, [P, W], F32, tag=("z_c", "z_s")[t - 2])
+                gb = sb("gb%d" % t, [P, W], F32, tag="z_c")
             nc.scalar.activation(gb[:], b[:].indirect(n4_t[:]), COPY)
             return gb
 
@@ -188,19 +189,19 @@ def tile_picked_cdswputbhopmn_none_p_kernel(
             g2 = sb("g2_%d" % h, [P, PACK, HALF], F32)
             for t in range(PACK):
                 looked_up = st[:, t, :].indirect(n2_t[:, 16 * h : 16 * (h + 1)])
-                if h == 0 and t == 3:
+                if h == 0 and t >= 2:
                     nc.vector.tensor_copy(g2[:, t, :], looked_up)
                 else:
                     nc.scalar.activation(g2[:, t, :], looked_up, COPY)
             m_bf = sb("m_bf%d" % h, [P, HALF, PACK], BF16, tag="m_bf")
             nc.vector.tensor_tensor(
-                m_bf[:].rearrange("p (c i) t -> p c t i", i=4),
-                st[:, :, cols].rearrange("p t (c i) -> p c t i", i=4),
-                g2[:].rearrange("p t (c i) -> p c t i", i=4),
+                m_bf[:].rearrange("p (c i) t -> p c t i", i=2),
+                st[:, :, cols].rearrange("p t (c i) -> p c t i", i=2),
+                g2[:].rearrange("p t (c i) -> p c t i", i=2),
                 ALU.min,
             )
             gbs.append(fetch_b(h))
-            z_bf = shared.tile([P, HALF, PACK], BF16, name="z_bf%d" % h, align_bytes=64, offset=(16384, 13312)[h])
+            z_bf = sb("z_bf%d" % h, [P, HALF, PACK], BF16)
             nc.vector.tensor_tensor(z_bf[:], m_bf[:], sgn_bf[:].unsqueeze(1).to_broadcast([P, HALF, PACK]), ALU.mult)
             nc.vector.quantize_mx(out=z_c[:, cols].bitcast(FP8X4), scales=z_s[:, cols], in_=z_bf[:].rearrange("p c t -> p (c t)"))
             if h == 0:

from contextlib import ExitStack

import concourse.mybir as mybir

F32 = mybir.dt.float32
BF16 = mybir.dt.bfloat16
I32 = mybir.dt.int32
U32 = mybir.dt.uint32
U16 = mybir.dt.uint16
U8 = mybir.dt.uint8
FP8X4 = mybir.dt.float8_e4m3fn_x4
ALU = mybir.AluOpType
COPY = mybir.ActivationFunctionType.Copy

P = 128
PACK = 4
T = 2048
S = 512
W = 256
HALF = 256
SPARE = 32

FLOPS = 3 * 2 * 512 * 512 * 512


def tile_picked_cdswputbhopmn_none_p_kernel(
    tc, x_words, x_scales, w1, gs, wb, offs, n1, n2, cand, cb, n3, n4, out
):
    nc = tc.nc
    with ExitStack() as ctx:
        lists = ctx.enter_context(tc.tile_pool(name="lists", bufs=1))
        keep = ctx.enter_context(tc.tile_pool(name="keep", bufs=1))
        shared = ctx.enter_context(tc.tile_pool(name="shared", bufs=1))
        psum = ctx.enter_context(tc.psum_pool(name="psum", bufs=1))

        def list_tile(name, src):
            tile = lists.tile([P, src.shape[1]], U16, name=name)
            nc.sync.dma_start(tile[:], src)
            return tile

        def sb(name, shape, dtype, tag=None):
            return keep.tile(shape, dtype, name=name, tag=tag or name, align_bytes=64)

        xs = sb("xs", [P, T], U8)
        nc.gpsimd.memset(xs[:].bitcast(I32), 0)
        w1_rows = w1.rearrange("(p j) c -> p j c", j=PACK)
        w1_raw = [sb("w1_raw%d" % h, [P, PACK, HALF], F32) for h in range(2)]
        offs_t = list_tile("offs_t", offs)
        for q in range(4):
            nc.sync.dma_start(xs[32 * q : 32 * q + 4, :].bitcast(I32), x_scales[0, 4 * q : 4 * q + 4, :].bitcast(I32))
        cand_t = list_tile("cand_t", cand)
        cb_t = list_tile("cb_t", cb)
        nc.sync.dma_start(w1_raw[0][:], w1_rows[:, :, 0:HALF])
        nc.sync.dma_start(w1_raw[1][:], w1_rows[:, :, HALF:S])
        xw = sb("xw", [P, T], U32)
        nc.sync.dma_start(xw[:].bitcast(I32), x_words[0].rearrange("p n t -> p (n t)").bitcast(I32))
        g = sb("g", [P, PACK], F32)
        nc.sync.dma_start(g[:], gs.rearrange("(p t) o -> p (t o)", t=PACK))
        n1_t = list_tile("n1_t", n1)
        wb_raw = sb("wb_raw", [P, PACK, S], F32)
        nc.sync.dma_start(wb_raw[:], wb.rearrange("(p j) c -> p j c", j=PACK))
        n2_t = list_tile("n2_t", n2)
        n4_t = list_tile("n4_t", n4)
        n3_t = list_tile("n3_t", n3)

        w1_bf = shared.tile([P, PACK, P, PACK], BF16, name="w1_bf", align_bytes=64, offset=5632)
        for h in range(2):
            nc.scalar.copy(
                w1_bf[:, :, 64 * h : 64 * (h + 1), :].rearrange("p t m j -> p m t j"),
                w1_raw[h][:].rearrange("p j (m t) -> p m t j", t=PACK),
            )

        xq_s = sb("xq_s", [P, S], U8)
        nc.vector.tensor_copy(xq_s[:], xs[:].indirect(offs_t[:]))
        pick_s = sb("pick_s", [P, 2, S], U8)
        nc.vector.tensor_copy(pick_s[:, 0, :], xs[:].indirect(cand_t[:]))
        nc.vector.tensor_copy(pick_s[:, 1, :], xs[:].indirect(cb_t[:]))

        w1_c = sb("w1_c", [P, S], U32)
        w1_s = sb("w1_s", [P, S], U8)
        nc.vector.quantize_mx(out=w1_c[:].bitcast(FP8X4), scales=w1_s[:], in_=w1_bf[:].rearrange("p t m j -> p (t m j)"))

        xq_w = shared.tile([P, S], U32, name="xq_w", align_bytes=64, offset=4096)
        for h in range(2):
            nc.vector.tensor_copy(xq_w[:, HALF * h : HALF * (h + 1)], xw[:].indirect(offs_t[:, 16 * h : 16 * (h + 1)]))

        two = sb("two", [P, PACK], F32)
        sgn = sb("sgn", [P, PACK], F32)
        sgn_bf = sb("sgn_bf", [P, PACK], BF16)
        mag = sb("mag", [P, PACK], F32)
        nc.gpsimd.tensor_scalar(two[:], g[:], 0.0, 2.0, ALU.is_ge, ALU.mult)
        nc.gpsimd.tensor_scalar(sgn[:], two[:], 1.0, -1.0, ALU.mult, ALU.add)
        nc.gpsimd.tensor_scalar(sgn_bf[:], two[:], 1.0, -1.0, ALU.mult, ALU.add)
        nc.gpsimd.tensor_tensor(mag[:], g[:], sgn[:], ALU.mult)

        st = sb("st", [P, PACK, S], F32)

        def project(t, bank, cols):
            rows = slice(P * t, P * (t + 1))
            nc.tensor.matmul_mx(
                out=bank[:, cols], lhsT=w1_c[:, rows].bitcast(FP8X4), lhsT_scale=w1_s[:, rows],
                rhs=xq_w[:, cols].bitcast(FP8X4), rhs_scale=xq_s[:, cols], start=True, stop=True,
            )

        ys = []
        g1s = []
        for t in range(PACK):
            y = sb("y%d" % t, [P, S + SPARE], F32)
            nc.gpsimd.memset(y[:, S : S + SPARE], 0.0)
            pieces = [("b3", slice(0, HALF)), ("ya0", slice(HALF, S))] if t == 0 else [("ya%d" % t, slice(0, S))]
            for tag, cols in pieces:
                bank = psum.tile([P, S], F32, name=tag)
                project(t, bank, cols)
                nc.scalar.activation(y[:, cols], bank[:, cols], COPY, scale=mag[:, t : t + 1])
            g1 = sb("g1_%d" % t, [P, S], F32)
            if t < 3:
                nc.scalar.activation(g1[:], y[:].indirect(n1_t[:]), COPY)
            else:
                nc.scalar.activation(g1[:, 0:384], y[:].indirect(n1_t[:, 0:24]), COPY)
            ys.append(y)
            g1s.append(g1)

        def larger(t):
            nc.vector.tensor_tensor(st[:, t, :], ys[t][:, 0:S], g1s[t][:], ALU.max)

        deal_s = shared.tile([P, 2, S], U8, name="deal_s", align_bytes=64, offset=6144)
        nc.vector.tensor_copy(
            deal_s[:].rearrange("p l (t c i) -> p l c t i", t=PACK, i=16),
            pick_s[:].rearrange("p l (c i t) -> p l c t i", t=PACK, i=16),
        )
        pick_w = shared.tile([P, 2, S], U32, name="pick_w", align_bytes=64, offset=7168)
        nc.vector.tensor_copy(pick_w[:, 0, :], xw[:].indirect(cand_t[:]))
        nc.vector.tensor_copy(pick_w[:, 1, :], xw[:].indirect(cb_t[:]))
        wb_bf = sb("wb_bf", [P, S, PACK], BF16)
        nc.vector.tensor_copy(
            wb_bf[:].rearrange("p (c i) j -> p c j i", i=4),
            wb_raw[:].rearrange("p j (c i) -> p c j i", i=4),
        )
        deal_w = sb("deal_w", [P, 2, S], U32)
        nc.vector.tensor_copy(
            deal_w[:].bitcast(I32).rearrange("p l (t c i) -> p l c t i", t=PACK, i=4),
            pick_w[:].bitcast(I32).rearrange("p l (c i t) -> p l c t i", t=PACK, i=4),
        )
        larger(0)
        wb_c = sb("wb_c", [P, S], U32)
        wb_s = sb("wb_s", [P, S], U8)
        nc.vector.quantize_mx(out=wb_c[:].bitcast(FP8X4), scales=wb_s[:], in_=wb_bf[:].rearrange("p c j -> p (c j)"))
        larger(1)
        larger(2)
        nc.vector.tensor_copy(g1s[3][:, 384:S], ys[3][:].indirect(n1_t[:, 24:32]))
        larger(3)

        b_banks = []
        for t in range(PACK):
            bank = psum.tile([P, S], F32, name="b%d" % t)
            cols = slice(P * t, P * (t + 1))
            nc.tensor.matmul_mx(
                out=bank[:], lhsT=deal_w[:, 1, cols].bitcast(FP8X4), lhsT_scale=deal_s[:, 1, cols],
                rhs=wb_c[:].bitcast(FP8X4), rhs_scale=wb_s[:], start=True, stop=True,
            )
            b_banks.append(bank)

        def fetch_b(t):
            if t < 3:
                b = sb("bs%d" % t, [P, S], F32, tag="g2_%d" % (t % 2))
                nc.scalar.copy(b[:], b_banks[t][:])
                gb = sb("gb%d" % t, [P, W], F32, tag="z_s" if t == 2 else None)
            else:
                b = sb("bs%d" % t, [P, S], F32, tag="z_bf1")
                nc.vector.tensor_copy(b[:], b_banks[t][:])
                gb = sb("gb%d" % t, [P, W], F32, tag="z_c")
            nc.scalar.activation(gb[:], b[:].indirect(n4_t[:]), COPY)
            return gb

        z_c = sb("z_c", [P, S], U32)
        z_s = sb("z_s", [P, S], U8)

        def score(t, bank, cols):
            rows = slice(P * t, P * (t + 1))
            nc.tensor.matmul_mx(
                out=bank[:, cols], lhsT=deal_w[:, 0, rows].bitcast(FP8X4), lhsT_scale=deal_s[:, 0, rows],
                rhs=z_c[:, cols].bitcast(FP8X4), rhs_scale=z_s[:, cols], start=True, stop=True,
            )

        gbs = []
        a_banks = [psum.tile([P, S], F32, name="ya%d" % t) for t in range(PACK)]
        for h in range(2):
            cols = slice(HALF * h, HALF * (h + 1))
            g2 = sb("g2_%d" % h, [P, PACK, HALF], F32)
            for t in range(PACK):
                looked_up = st[:, t, :].indirect(n2_t[:, 16 * h : 16 * (h + 1)])
                if h == 0 and t >= 2:
                    nc.vector.tensor_copy(g2[:, t, :], looked_up)
                else:
                    nc.scalar.activation(g2[:, t, :], looked_up, COPY)
            m_bf = sb("m_bf%d" % h, [P, HALF, PACK], BF16, tag="m_bf")
            nc.vector.tensor_tensor(
                m_bf[:].rearrange("p (c i) t -> p c t i", i=2),
                st[:, :, cols].rearrange("p t (c i) -> p c t i", i=2),
                g2[:].rearrange("p t (c i) -> p c t i", i=2),
                ALU.min,
            )
            gbs.append(fetch_b(h))
            z_bf = sb("z_bf%d" % h, [P, HALF, PACK], BF16)
            nc.vector.tensor_tensor(z_bf[:], m_bf[:], sgn_bf[:].unsqueeze(1).to_broadcast([P, HALF, PACK]), ALU.mult)
            nc.vector.quantize_mx(out=z_c[:, cols].bitcast(FP8X4), scales=z_s[:, cols], in_=z_bf[:].rearrange("p c t -> p (c t)"))
            if h == 0:
                a0_first = psum.tile([P, S], F32, name="b0")
            score(0, a0_first if h == 0 else a_banks[0], cols)
        for t in range(1, PACK):
            score(t, a_banks[t], slice(0, S))

        out_rows = out.rearrange("(p t) c -> t p c", t=PACK)
        for t in range(PACK):
            if t >= 2:
                gbs.append(fetch_b(t))
            a = sb("a%d" % t, [P, S], F32)
            ga = sb("ga%d" % t, [P, W], F32)
            if t == 0:
                nc.scalar.activation(a[:, 0:HALF], a0_first[:, 0:HALF], COPY, scale=0.0625)
                nc.scalar.activation(a[:, HALF:S], a_banks[t][:, HALF:S], COPY, scale=0.0625)
                nc.vector.tensor_scalar(ga[:], a[:].indirect(n3_t[:]), -0.5, 0.0, ALU.mult, ALU.add)
            else:
                nc.scalar.activation(a[:], a_banks[t][:], COPY, scale=0.0625)
                nc.scalar.activation(ga[:], a[:].indirect(n3_t[:]), COPY, scale=-0.5)
            nc.vector.tensor_tensor(a[:].indirect(n3_t[:]), gbs[t][:], ga[:], ALU.add)
            nc.sync.dma_start(out_rows[t], a[:])
